import numpy as np
import ml_dtypes


def mxq(x, axis, fmt="e4m3"):
    dtype, down = {"e4m3": (ml_dtypes.float8_e4m3fn, 7), "e5m2": (ml_dtypes.float8_e5m2, 14)}[fmt]
    v = np.moveaxis(np.asarray(x, np.float32).astype(ml_dtypes.bfloat16).astype(np.float64), axis, -1)
    blocks = v.reshape(v.shape[:-1] + (-1, 32))
    amax = np.abs(blocks).max(-1, keepdims=True)
    byte = np.maximum(np.where(amax > 0, np.frexp(amax)[1] - 1 + 127, 0) - down, 1)
    scale = np.exp2(byte - 127.0)
    codes = (blocks / scale).astype(np.float32).astype(dtype).astype(np.float64)
    return np.moveaxis((codes * scale).reshape(v.shape), -1, axis)


WIDE = False


def mx_kscale(k):
    if not WIDE:
        return np.ones(k)
    levels = np.array([10, -10, 5, -5, 0])
    if k % 512:
        return np.exp2(np.random.permutation(np.resize(levels, k // 32))).repeat(32)
    a = np.empty((k // 512, 16))
    for p in range(k // 512):
        a[p, :8] = np.random.permutation(np.resize(levels, 8))
        for g in range(8):
            far = levels[np.abs(levels - a[p, g]) >= 10]
            a[p, g + 8] = far[np.random.randint(len(far))]
    return np.exp2(a.ravel()).repeat(32)


def f64(x):
    return np.asarray(x).astype(np.float64)


def striped(idx):
    return np.tile(idx.reshape(-1, 16).T, (8, 1)).astype(np.uint16)


def unstriped(offs):
    return offs[:16].T.reshape(-1).astype(np.int64)


E2M1 = np.array([0.0, 0.5, 1.0, 1.5, 2.0, 3.0, 4.0, 6.0, -0.0, -0.5, -1.0, -1.5, -2.0, -3.0, -4.0, -6.0])


def pack_fp4(w):
    k, n = w.shape
    w = f64(np.asarray(w, np.float32).astype(ml_dtypes.bfloat16)).reshape(k // 32, 32, n)
    amax = np.abs(w).max(1)
    mant, ex = np.frexp(amax / 6.0)
    byte = np.clip(np.where(amax > 0, np.where(mant > 0.5, ex, ex - 1) + 127, 1), 1, 254)
    scaled = (w * np.exp2(127.0 - byte)[:, None, :]).reshape(k, n).astype(np.float32)
    c = np.ascontiguousarray(scaled.reshape(k // 512, 128, 4, n).transpose(0, 1, 3, 2)).astype(ml_dtypes.float4_e2m1fn).view(np.uint8) & 0xF
    words = (c[..., 0::2] | (c[..., 1::2] << 4)).reshape(k // 512, 128, 2 * n)
    return np.ascontiguousarray(words), np.ascontiguousarray(byte.astype(np.uint8).reshape(k // 512, 16, n))


def unpack_fp4(words, scales):
    g, _, n = scales.shape
    words = np.ascontiguousarray(words).reshape(g, 128, n, 2)
    nib = np.empty((g, 128, n, 4), np.uint8)
    nib[..., 0::2] = words & 0xF
    nib[..., 1::2] = words >> 4
    vals = E2M1[nib] * np.repeat(np.exp2(scales.astype(np.float64) - 127.0), 8, axis=1)[..., None]
    return vals.transpose(0, 1, 3, 2).reshape(g * 512, n)


K, T, S, N, U = 512, 2048, 1024, 256, 2048
P = 2 ** 7


def setup_inputs():
    n = np.random.standard_normal
    s = mx_kscale(K)[:, None]
    packed_w1 = pack_fp4(n((K, N)) / np.sqrt(K) / s)
    return {
        "xT": (n((K, T)) * s).astype(np.float32),
        "mem": n((N, U)).astype(np.float32),
        "w1_words": packed_w1[0],
        "w1_scales": packed_w1[1],
        "old": np.tile(np.random.uniform(0.5, 0.95, S), (P, 1)).astype(np.float32),
        "new": np.tile(np.random.uniform(0.05, 0.5, S), (P, 1)).astype(np.float32),
        "offs": striped(np.random.permutation(T)[:S]),
        "slot": striped(np.random.permutation(U)[:S]),
    }


def reference(xT, mem, w1_words, w1_scales, old, new, offs, slot):
    xq = mxq(f64(xT)[:, unstriped(offs)], 0, "e4m3")
    y = unpack_fp4(w1_words, w1_scales).T @ xq
    out = f64(mem).copy()
    out[:, unstriped(slot)] = f64(mem)[:, unstriped(slot)] * f64(old)[:1] + y * f64(new)[:1]
    return out

@@ -1,0 +1,169 @@
+from contextlib import ExitStack
+
+import concourse.mybir as mybir
+from concourse.masks import make_identity
+
+K, T, S, N, U = 512, 2048, 1024, 256, 2048
+P = 128
+PACK = 4
+BANK = 512
+FLOPS = 2 * K * N * S
+
+F32 = mybir.dt.float32
+BF16 = mybir.dt.bfloat16
+I32 = mybir.dt.int32
+U32 = mybir.dt.uint32
+U16 = mybir.dt.uint16
+U8 = mybir.dt.uint8
+FP8X4 = mybir.dt.float8_e4m3fn_x4
+FP4X4 = mybir.dt.float4_e2m1fn_x4
+MULT = mybir.AluOpType.mult
+ADD = mybir.AluOpType.add
+COPY = mybir.ActivationFunctionType.Copy
+
+CHUNKS = ((0, 0, 1024, 1024), (0, 1024, 1024, 384), (1, 0, 1024, 512), (1, 1024, 512, 512), (1, 1536, 256, 0), (1, 1792, 256, 0))
+SLICES = ((0, 256), (256, 256), (512, 512))
+
+
+def tile_picked_ema_none_e_kernel(tc, xT, mem, w1_words, w1_scales, old, new, offs, slot, out):
+    nc = tc.nc
+    blocks = N // P
+    with ExitStack() as ctx:
+        keep = ctx.enter_context(tc.tile_pool(name="keep", bufs=1))
+        ring = ctx.enter_context(tc.psum_pool(name="ring", bufs=3))
+
+        slot_sb = keep.tile([P, S // 16], U16, name="slot_sb")
+        offs_sb = keep.tile([P, S // 16], U16, name="offs_sb")
+        mem_sb = [keep.tile([P, U], F32, name=f"mem{b}") for b in range(blocks)]
+        old_cols = keep.tile([P, S // BANK, 4], F32, name="old_cols")
+        new_rows = keep.tile([P, P], F32, name="new_rows")
+        w_words = keep.tile([P, 2 * N], U8, name="w_words", align_bytes=64)
+        w_scales = keep.tile([P, N], U8, name="w_scales", align_bytes=64)
+        x_rows = xT.rearrange("(p j) t -> p j t", j=PACK)
+        raws = [keep.tile([P, 2, chunk[2]], F32, name=f"raw{i}") for i, chunk in enumerate(CHUNKS)]
+
+        def load_x(i):
+            u, c0, cols, unused = CHUNKS[i]
+            nc.sync.dma_start(raws[i][:], x_rows[:, 2 * u : 2 * u + 2, c0 : c0 + cols])
+
+        def load_scales(q):
+            nc.sync.dma_start(w_scales[32 * q : 32 * q + 4, :].bitcast(I32), w1_scales[0, 4 * q : 4 * q + 4, :].bitcast(I32))
+
+        nc.gpsimd.memset(w_scales[:].bitcast(I32), 0)
+        nc.sync.dma_start(old_cols[:], old[0:1, :].rearrange("o (h p u) -> p (o h) u", p=P, u=4))
+        nc.sync.dma_start(mem_sb[0][:], mem[0:P, :])
+        nc.sync.dma_start(slot_sb[:], slot)
+        nc.sync.dma_start(offs_sb[:], offs)
+        load_x(0)
+        nc.sync.dma_start(w_words[:].bitcast(I32), w1_words[0].bitcast(I32))
+        load_x(1)
+        for q in range(3):
+            load_scales(q)
+        load_x(2)
+        load_scales(3)
+        nc.sync.dma_start(new_rows[:], new.rearrange("r (u c) -> (r u) c", c=P)[0:P, :])
+        for i in range(3, len(CHUNKS)):
+            load_x(i)
+        nc.sync.dma_start(mem_sb[1][:], mem[P : 2 * P, :])
+
+        ident = keep.tile([P, P], F32, name="ident")
+        make_identity(nc, ident[:])
+
+        old_wide = keep.tile([P, S // P, P], F32, name="old_wide")
+        nc.vector.tensor_copy(old_wide[:], old_cols[:].rearrange("p h u -> p (h u)").unsqueeze(2).to_broadcast([P, S // P, P]))
+        old_sb = keep.tile([P, S], F32, name="old_sb")
+        for h in range(S // BANK):
+            bank = ring.tile([P, 4, P], F32, name="bank")
+            for u in range(4):
+                nc.tensor.transpose(bank[:, u, :], old_wide[:, 4 * h + u, :], ident[:])
+            dst = old_sb[:, h * BANK : (h + 1) * BANK].rearrange("p (n u) -> p n u", u=4)
+            src = bank[:].rearrange("p u n -> p n u")
+            nc.vector.tensor_copy(dst, src)
+
+        kept = [keep.tile([P, S], F32, name=f"kept{b}") for b in range(blocks)]
+
+        def gather_mem(b, j0, n):
+            lst = slot_sb[:, j0 // 16 : (j0 + n) // 16]
+            nc.vector.tensor_tensor(kept[b][:, j0 : j0 + n], mem_sb[b][:].indirect(lst), old_sb[:, j0 : j0 + n], MULT)
+
+        pairs = [keep.tile([P, T, 2], BF16, name=f"pairs{u}") for u in range(2)]
+        picked = [keep.tile([P, 2, n], U32, name=f"picked{s}") for s, (j0, n) in enumerate(SLICES)]
+
+        def round_chunk(i):
+            u, c0, cols, s_cols = CHUNKS[i]
+            src = raws[i][:].rearrange("p e c -> p c e")
+            if s_cols > 0:
+                nc.scalar.copy(pairs[u][:, c0 : c0 + s_cols, :], src[:, 0:s_cols, :])
+            if s_cols < cols:
+                nc.vector.tensor_copy(pairs[u][:, c0 + s_cols : c0 + cols, :], src[:, s_cols:cols, :])
+
+        def gather_pairs(u):
+            window = pairs[u][:].rearrange("p t e -> p (t e)").bitcast(U32)
+            for s, (j0, n) in enumerate(SLICES):
+                nc.vector.tensor_copy(picked[s][:, u, :], window.indirect(offs_sb[:, j0 // 16 : (j0 + n) // 16]))
+
+        gather_mem(0, 0, S)
+        round_chunk(0)
+        round_chunk(1)
+        gather_pairs(0)
+
+        new_cols = keep.tile([P, S // P], F32, name="new_cols")
+        bank = ring.tile([P, 4, P], F32, name="bank")
+        nc.tensor.transpose(bank[:, 0, :], new_rows[:], ident[:])
+        nc.scalar.copy(new_cols[:], bank[:, 0, 0 : S // P])
+
+        for i in range(2, len(CHUNKS)):
+            round_chunk(i)
+        gather_pairs(1)
+
+        codes = []
+        for s, (j0, n) in enumerate(SLICES):
+            grouped = keep.tile([P, PACK * n], BF16, name=f"grouped{s}", align_bytes=64)
+            nc.scalar.copy(grouped[:].bitcast(U32).rearrange("p (c u) -> p c u", u=2), picked[s][:].rearrange("p u c -> p c u"))
+            pw = keep.tile([P, n], U32, name=f"pw{s}", align_bytes=64)
+            ps = keep.tile([P, n], U8, name=f"ps{s}", align_bytes=64)
+            if s == len(SLICES) - 1:
+                gather_mem(1, 0, S // 2)
+            nc.vector.quantize_mx(out=pw[:].bitcast(FP8X4), scales=ps[:], in_=grouped[:])
+            codes.append((pw, ps))
+        gather_mem(1, S // 2, S // 2)
+
+        updates = []
+        for s, (j0, n) in enumerate(SLICES):
+            pw, ps = codes[s]
+            scaled = keep.tile([P, n // P, N], F32, name=f"scaled{s}")
+            for pair in range(n // (2 * P)):
+                bank = ring.tile([P, 4, P], F32, name="bank")
+                acc = bank[:].rearrange("p (e b) m -> p e (b m)", e=2)
+                for e in range(2):
+                    t = 2 * pair + e
+                    nc.tensor.matmul_mx(
+                        out=acc[:, e, :],
+                        lhsT=pw[:, P * t : P * (t + 1)].bitcast(FP8X4),
+                        lhsT_scale=ps[:, P * t : P * (t + 1)],
+                        rhs=w_words[:].bitcast(FP4X4),
+                        rhs_scale=w_scales[:],
+                        start=True,
+                        stop=True,
+                    )
+                for e in range(2):
+                    t = 2 * pair + e
+                    col = j0 // P + t
+                    nc.scalar.activation(scaled[:, t, :], acc[:, e, :], COPY, scale=new_cols[:, col : col + 1])
+            fresh = keep.tile([P, blocks, n], F32, name=f"fresh{s}")
+            per_bank = BANK // n
+            for g in range(blocks // per_bank):
+                turned = ring.tile([P, per_bank, n], F32, name="bank")
+                for i in range(per_bank):
+                    b = g * per_bank + i
+                    for t in range(n // P):
+                        nc.tensor.transpose(turned[:, i, P * t : P * (t + 1)], scaled[:, t, P * b : P * (b + 1)], ident[:])
+                nc.scalar.copy(fresh[:, g * per_bank : (g + 1) * per_bank, :], turned[:])
+            updates.append(fresh)
+
+        for s, (j0, n) in enumerate(SLICES):
+            lst = slot_sb[:, j0 // 16 : (j0 + n) // 16]
+            for b in range(blocks):
+                nc.vector.tensor_tensor(mem_sb[b][:].indirect(lst), kept[b][:, j0 : j0 + n], updates[s][:, b, :], ADD)
+        for b in range(blocks):
+            nc.sync.dma_start(out[P * b : P * (b + 1), :], mem_sb[b][:])

@@ -18,7 +18,6 @@ U8 = mybir.dt.uint8
 FP8X4 = mybir.dt.float8_e4m3fn_x4
 FP4X4 = mybir.dt.float4_e2m1fn_x4
 MULT = mybir.AluOpType.mult
-ADD = mybir.AluOpType.add
 COPY = mybir.ActivationFunctionType.Copy
 
 CHUNKS = ((0, 0, 1024, 1024), (0, 1024, 1024, 384), (1, 0, 1024, 512), (1, 1024, 512, 512), (1, 1536, 256, 0), (1, 1792, 256, 0))
@@ -30,13 +29,15 @@ def tile_picked_ema_none_e_kernel(tc, xT, mem, w1_words, w1_scales, old, new, of
     blocks = N // P
     with ExitStack() as ctx:
         keep = ctx.enter_context(tc.tile_pool(name="keep", bufs=1))
-        ring = ctx.enter_context(tc.psum_pool(name="ring", bufs=3))
+        psum = ctx.enter_context(tc.psum_pool(name="psum", bufs=1))
+
+        def bank(i):
+            return psum.tile([P, 4, P], F32, name=f"bank{i}")
 
         slot_sb = keep.tile([P, S // 16], U16, name="slot_sb")
         offs_sb = keep.tile([P, S // 16], U16, name="offs_sb")
         mem_sb = [keep.tile([P, U], F32, name=f"mem{b}") for b in range(blocks)]
-        old_cols = keep.tile([P, S // BANK, 4], F32, name="old_cols")
-        new_rows = keep.tile([P, P], F32, name="new_rows")
+        weight_rows = keep.tile([P, P], F32, name="weight_rows")
         w_words = keep.tile([P, 2 * N], U8, name="w_words", align_bytes=64)
         w_scales = keep.tile([P, N], U8, name="w_scales", align_bytes=64)
         x_rows = xT.rearrange("(p j) t -> p j t", j=PACK)
@@ -50,9 +51,10 @@ def tile_picked_ema_none_e_kernel(tc, xT, mem, w1_words, w1_scales, old, new, of
             nc.sync.dma_start(w_scales[32 * q : 32 * q + 4, :].bitcast(I32), w1_scales[0, 4 * q : 4 * q + 4, :].bitcast(I32))
 
         nc.gpsimd.memset(w_scales[:].bitcast(I32), 0)
-        nc.sync.dma_start(old_cols[:], old[0:1, :].rearrange("o (h p u) -> p (o h) u", p=P, u=4))
-        nc.sync.dma_start(mem_sb[0][:], mem[0:P, :])
         nc.sync.dma_start(slot_sb[:], slot)
+        nc.sync.dma_start(mem_sb[0][:], mem[0:P, :])
+        for a, weight in enumerate((new, old)):
+            nc.sync.dma_start(weight_rows[64 * a : 64 * (a + 1), :], weight.rearrange("r (u c) -> (r u) c", c=P)[0:64, :])
         nc.sync.dma_start(offs_sb[:], offs)
         load_x(0)
         nc.sync.dma_start(w_words[:].bitcast(I32), w1_words[0].bitcast(I32))
@@ -61,7 +63,6 @@ def tile_picked_ema_none_e_kernel(tc, xT, mem, w1_words, w1_scales, old, new, of
             load_scales(q)
         load_x(2)
         load_scales(3)
-        nc.sync.dma_start(new_rows[:], new.rearrange("r (u c) -> (r u) c", c=P)[0:P, :])
         for i in range(3, len(CHUNKS)):
             load_x(i)
         nc.sync.dma_start(mem_sb[1][:], mem[P : 2 * P, :])
@@ -69,25 +70,30 @@ def tile_picked_ema_none_e_kernel(tc, xT, mem, w1_words, w1_scales, old, new, of
         ident = keep.tile([P, P], F32, name="ident")
         make_identity(nc, ident[:])
 
-        old_wide = keep.tile([P, S // P, P], F32, name="old_wide")
-        nc.vector.tensor_copy(old_wide[:], old_cols[:].rearrange("p h u -> p (h u)").unsqueeze(2).to_broadcast([P, S // P, P]))
-        old_sb = keep.tile([P, S], F32, name="old_sb")
-        for h in range(S // BANK):
-            bank = ring.tile([P, 4, P], F32, name="bank")
-            for u in range(4):
-                nc.tensor.transpose(bank[:, u, :], old_wide[:, 4 * h + u, :], ident[:])
-            dst = old_sb[:, h * BANK : (h + 1) * BANK].rearrange("p (n u) -> p n u", u=4)
-            src = bank[:].rearrange("p u n -> p n u")
-            nc.vector.tensor_copy(dst, src)
+        weight_cols = keep.tile([P, 2, S // P], F32, name="weight_cols")
+        turned_weights = bank(0)
+        nc.tensor.transpose(turned_weights[:, 0, :], weight_rows[:], ident[:])
+        nc.vector.tensor_copy(weight_cols[:], turned_weights[:, 0, :].rearrange("p (a c) -> p a c", a=2)[:, :, 0 : S // P])
 
-        kept = [keep.tile([P, S], F32, name=f"kept{b}") for b in range(blocks)]
+        kept = [[keep.tile([P, 4, P], F32, name=f"kept{b}{h}") for h in range(S // BANK)] for b in range(blocks)]
 
-        def gather_mem(b, j0, n):
-            lst = slot_sb[:, j0 // 16 : (j0 + n) // 16]
-            nc.vector.tensor_tensor(kept[b][:, j0 : j0 + n], mem_sb[b][:].indirect(lst), old_sb[:, j0 : j0 + n], MULT)
+        def gather_mem(b, h):
+            looked = keep.tile([P, BANK], F32, name=f"looked{b}{h}")
+            nc.vector.tensor_copy(looked[:], mem_sb[b][:].indirect(slot_sb[:, h * BANK // 16 : (h + 1) * BANK // 16]))
+            return looked
+
+        def weigh_mem(b, h, looked, turned):
+            for t in range(4):
+                nc.tensor.transpose(turned[:, t, :], looked[:, P * t : P * (t + 1)], ident[:])
+            old_cols = weight_cols[:, 1, 4 * h : 4 * h + 4]
+            if b == 0:
+                nc.vector.tensor_tensor(kept[b][h][:], turned[:], old_cols.unsqueeze(2).to_broadcast([P, 4, P]), MULT)
+            else:
+                for t in range(4):
+                    nc.scalar.activation(kept[b][h][:, t, :], turned[:, t, :], COPY, scale=old_cols[:, t : t + 1])
 
         pairs = [keep.tile([P, T, 2], BF16, name=f"pairs{u}") for u in range(2)]
-        picked = [keep.tile([P, 2, n], U32, name=f"picked{s}") for s, (j0, n) in enumerate(SLICES)]
+        picked = [keep.tile([P, 2 * n], U32, name=f"picked{s}", align_bytes=64) for s, (j0, n) in enumerate(SLICES)]
 
         def round_chunk(i):
             u, c0, cols, s_cols = CHUNKS[i]
@@ -97,73 +103,83 @@ def tile_picked_ema_none_e_kernel(tc, xT, mem, w1_words, w1_scales, old, new, of
             if s_cols < cols:
                 nc.vector.tensor_copy(pairs[u][:, c0 + s_cols : c0 + cols, :], src[:, s_cols:cols, :])
 
-        def gather_pairs(u):
+        def gather_pairs(u, s):
+            j0, n = SLICES[s]
             window = pairs[u][:].rearrange("p t e -> p (t e)").bitcast(U32)
-            for s, (j0, n) in enumerate(SLICES):
-                nc.vector.tensor_copy(picked[s][:, u, :], window.indirect(offs_sb[:, j0 // 16 : (j0 + n) // 16]))
+            nc.vector.tensor_copy(picked[s][:, u * n : (u + 1) * n], window.indirect(offs_sb[:, j0 // 16 : (j0 + n) // 16]))
 
-        gather_mem(0, 0, S)
+        first = [gather_mem(0, h) for h in range(2)]
+        for h in range(2):
+            weigh_mem(0, h, first[h], bank(1 + h))
         round_chunk(0)
         round_chunk(1)
-        gather_pairs(0)
-
-        new_cols = keep.tile([P, S // P], F32, name="new_cols")
-        bank = ring.tile([P, 4, P], F32, name="bank")
-        nc.tensor.transpose(bank[:, 0, :], new_rows[:], ident[:])
-        nc.scalar.copy(new_cols[:], bank[:, 0, 0 : S // P])
+        for s in range(len(SLICES)):
+            gather_pairs(0, s)
 
         for i in range(2, len(CHUNKS)):
             round_chunk(i)
-        gather_pairs(1)
 
-        codes = []
-        for s, (j0, n) in enumerate(SLICES):
-            grouped = keep.tile([P, PACK * n], BF16, name=f"grouped{s}", align_bytes=64)
-            nc.scalar.copy(grouped[:].bitcast(U32).rearrange("p (c u) -> p c u", u=2), picked[s][:].rearrange("p u c -> p c u"))
+        def quantize(s, woven):
+            j0, n = SLICES[s]
+            nc.scalar.copy(woven.rearrange("p (c u) -> p c u", u=2), picked[s][:].rearrange("p (u c) -> p c u", u=2))
             pw = keep.tile([P, n], U32, name=f"pw{s}", align_bytes=64)
             ps = keep.tile([P, n], U8, name=f"ps{s}", align_bytes=64)
-            if s == len(SLICES) - 1:
-                gather_mem(1, 0, S // 2)
-            nc.vector.quantize_mx(out=pw[:].bitcast(FP8X4), scales=ps[:], in_=grouped[:])
-            codes.append((pw, ps))
-        gather_mem(1, S // 2, S // 2)
+            nc.vector.quantize_mx(out=pw[:].bitcast(FP8X4), scales=ps[:], in_=woven.bitcast(BF16))
+            return pw, ps
+
+        scaled = [keep.tile([P, N], F32, name=f"scaled{t}") for t in range(S // P)]
+
+        def project(t0, pw, ps, first_col, target):
+            acc = target[:].rearrange("p (e b) m -> p e (b m)", e=2)
+            for e in range(2):
+                cols = slice(first_col + P * e, first_col + P * (e + 1))
+                nc.tensor.matmul_mx(
+                    out=acc[:, e, :],
+                    lhsT=pw[:, cols].bitcast(FP8X4),
+                    lhsT_scale=ps[:, cols],
+                    rhs=w_words[:].bitcast(FP4X4),
+                    rhs_scale=w_scales[:],
+                    start=True,
+                    stop=True,
+                )
+            for e in range(2):
+                nc.scalar.activation(scaled[t0 + e][:], acc[:, e, :], COPY, scale=weight_cols[:, 0, t0 + e : t0 + e + 1])
+
+        def combine(b, t0, tiles, total):
+            old_terms = [kept[b][(t0 + i) // 4][:, (t0 + i) % 4, :] for i in range(tiles)]
+            new_terms = [scaled[t0 + i][:, P * b : P * (b + 1)] for i in range(tiles)]
+            terms = old_terms + new_terms if b == 0 else new_terms + old_terms
+            for i, term in enumerate(terms):
+                nc.tensor.matmul(total[:, i % tiles, :], term, ident[:], start=(i == 0), stop=(i == len(terms) - 1), is_transpose=True)
+            update = keep.tile([P, tiles * P], F32, name=f"update{b}{t0}")
+            nc.scalar.copy(update[:], total[:, 0:tiles, :].rearrange("p i j -> p (i j)"))
+            return b, t0, tiles, update
+
+        woven = [keep.tile([P, 2 * n], U32, name=f"woven{s}", align_bytes=64) for s, (j0, n) in enumerate(SLICES)]
+        for s in range(len(SLICES)):
+            gather_pairs(1, s)
+        codes_a = quantize(0, woven[0][:])
+        codes_b = quantize(1, woven[1][:])
+        looked_0 = gather_mem(1, 0)
+        looked_1 = gather_mem(1, 1)
+        codes_c = quantize(2, woven[2][:])
 
         updates = []
-        for s, (j0, n) in enumerate(SLICES):
-            pw, ps = codes[s]
-            scaled = keep.tile([P, n // P, N], F32, name=f"scaled{s}")
-            for pair in range(n // (2 * P)):
-                bank = ring.tile([P, 4, P], F32, name="bank")
-                acc = bank[:].rearrange("p (e b) m -> p e (b m)", e=2)
-                for e in range(2):
-                    t = 2 * pair + e
-                    nc.tensor.matmul_mx(
-                        out=acc[:, e, :],
-                        lhsT=pw[:, P * t : P * (t + 1)].bitcast(FP8X4),
-                        lhsT_scale=ps[:, P * t : P * (t + 1)],
-                        rhs=w_words[:].bitcast(FP4X4),
-                        rhs_scale=w_scales[:],
-                        start=True,
-                        stop=True,
-                    )
-                for e in range(2):
-                    t = 2 * pair + e
-                    col = j0 // P + t
-                    nc.scalar.activation(scaled[:, t, :], acc[:, e, :], COPY, scale=new_cols[:, col : col + 1])
-            fresh = keep.tile([P, blocks, n], F32, name=f"fresh{s}")
-            per_bank = BANK // n
-            for g in range(blocks // per_bank):
-                turned = ring.tile([P, per_bank, n], F32, name="bank")
-                for i in range(per_bank):
-                    b = g * per_bank + i
-                    for t in range(n // P):
-                        nc.tensor.transpose(turned[:, i, P * t : P * (t + 1)], scaled[:, t, P * b : P * (b + 1)], ident[:])
-                nc.scalar.copy(fresh[:, g * per_bank : (g + 1) * per_bank, :], turned[:])
-            updates.append(fresh)
+        project(0, *codes_a, 0, bank(0))
+        updates.append(combine(0, 0, 2, bank(1)))
+        project(2, *codes_b, 0, bank(2))
+        updates.append(combine(0, 2, 2, bank(3)))
+        weigh_mem(1, 0, looked_0, bank(1))
+        updates.append(combine(1, 0, 4, bank(4)))
+        project(4, *codes_c, 0, bank(3))
+        project(6, *codes_c, 2 * P, bank(0))
+        updates.append(combine(0, 4, 4, bank(5)))
+        weigh_mem(1, 1, looked_1, bank(4))
+        updates.append(combine(1, 4, 4, bank(6)))
 
-        for s, (j0, n) in enumerate(SLICES):
-            lst = slot_sb[:, j0 // 16 : (j0 + n) // 16]
-            for b in range(blocks):
-                nc.vector.tensor_tensor(mem_sb[b][:].indirect(lst), kept[b][:, j0 : j0 + n], updates[s][:, b, :], ADD)
-        for b in range(blocks):
-            nc.sync.dma_start(out[P * b : P * (b + 1), :], mem_sb[b][:])
+        for b, t0, tiles, update in updates:
+            lst = slot_sb[:, t0 * P // 16 : (t0 + tiles) * P // 16]
+            nc.vector.tensor_copy(mem_sb[b][:].indirect(lst), update[:])
+        nc.sync.dma_start(out[0:P, :], mem_sb[0][:])
+        nc.sync.dma_start(out[P : 2 * P, 0 : U // 2], mem_sb[1][:, 0 : U // 2])
+        nc.scalar.dma_start(out[P : 2 * P, U // 2 : U], mem_sb[1][:, U // 2 : U])

@@ -20,7 +20,7 @@ FP4X4 = mybir.dt.float4_e2m1fn_x4
 MULT = mybir.AluOpType.mult
 COPY = mybir.ActivationFunctionType.Copy
 
-CHUNKS = ((0, 0, 1024, 1024), (0, 1024, 1024, 384), (1, 0, 1024, 512), (1, 1024, 512, 512), (1, 1536, 256, 0), (1, 1792, 256, 0))
+CHUNKS = ((0, 0, 1024, 1024), (0, 1024, 512, 0), (0, 1536, 512, 192), (1, 0, 512, 512), (1, 512, 512, 512), (1, 1024, 512, 256), (1, 1536, 256, 0), (1, 1792, 256, 96))
 SLICES = ((0, 256), (256, 256), (512, 512))
 
 
@@ -51,20 +51,20 @@ def tile_picked_ema_none_e_kernel(tc, xT, mem, w1_words, w1_scales, old, new, of
             nc.sync.dma_start(w_scales[32 * q : 32 * q + 4, :].bitcast(I32), w1_scales[0, 4 * q : 4 * q + 4, :].bitcast(I32))
 
         nc.gpsimd.memset(w_scales[:].bitcast(I32), 0)
-        nc.sync.dma_start(slot_sb[:], slot)
         nc.sync.dma_start(mem_sb[0][:], mem[0:P, :])
+        nc.sync.dma_start(slot_sb[:], slot)
         for a, weight in enumerate((new, old)):
             nc.sync.dma_start(weight_rows[64 * a : 64 * (a + 1), :], weight.rearrange("r (u c) -> (r u) c", c=P)[0:64, :])
         nc.sync.dma_start(offs_sb[:], offs)
         load_x(0)
-        nc.sync.dma_start(w_words[:].bitcast(I32), w1_words[0].bitcast(I32))
+        load_scales(0)
         load_x(1)
-        for q in range(3):
-            load_scales(q)
         load_x(2)
-        load_scales(3)
+        for q in range(1, 4):
+            load_scales(q)
         for i in range(3, len(CHUNKS)):
             load_x(i)
+        nc.sync.dma_start(w_words[:].bitcast(I32), w1_words[0].bitcast(I32))
         nc.sync.dma_start(mem_sb[1][:], mem[P : 2 * P, :])
 
         ident = keep.tile([P, P], F32, name="ident")
@@ -113,10 +113,11 @@ def tile_picked_ema_none_e_kernel(tc, xT, mem, w1_words, w1_scales, old, new, of
             weigh_mem(0, h, first[h], bank(1 + h))
         round_chunk(0)
         round_chunk(1)
+        round_chunk(2)
         for s in range(len(SLICES)):
             gather_pairs(0, s)
 
-        for i in range(2, len(CHUNKS)):
+        for i in range(3, len(CHUNKS)):
             round_chunk(i)
 
         def quantize(s, woven):

from contextlib import ExitStack

import concourse.mybir as mybir
from concourse.masks import make_identity

K, T, S, N, U = 512, 2048, 1024, 256, 2048
P = 128
PACK = 4
BANK = 512
FLOPS = 2 * K * N * S

F32 = mybir.dt.float32
BF16 = mybir.dt.bfloat16
I32 = mybir.dt.int32
U32 = mybir.dt.uint32
U16 = mybir.dt.uint16
U8 = mybir.dt.uint8
FP8X4 = mybir.dt.float8_e4m3fn_x4
FP4X4 = mybir.dt.float4_e2m1fn_x4
MULT = mybir.AluOpType.mult
COPY = mybir.ActivationFunctionType.Copy

CHUNKS = ((0, 0, 1024, 1024), (0, 1024, 512, 0), (0, 1536, 512, 192), (1, 0, 512, 512), (1, 512, 512, 512), (1, 1024, 512, 256), (1, 1536, 256, 0), (1, 1792, 256, 96))
SLICES = ((0, 256), (256, 256), (512, 512))


def tile_picked_ema_none_e_kernel(tc, xT, mem, w1_words, w1_scales, old, new, offs, slot, out):
    nc = tc.nc
    blocks = N // P
    with ExitStack() as ctx:
        keep = ctx.enter_context(tc.tile_pool(name="keep", bufs=1))
        psum = ctx.enter_context(tc.psum_pool(name="psum", bufs=1))

        def bank(i):
            return psum.tile([P, 4, P], F32, name=f"bank{i}")

        slot_sb = keep.tile([P, S // 16], U16, name="slot_sb")
        offs_sb = keep.tile([P, S // 16], U16, name="offs_sb")
        mem_sb = [keep.tile([P, U], F32, name=f"mem{b}") for b in range(blocks)]
        weight_rows = keep.tile([P, P], F32, name="weight_rows")
        w_words = keep.tile([P, 2 * N], U8, name="w_words", align_bytes=64)
        w_scales = keep.tile([P, N], U8, name="w_scales", align_bytes=64)
        x_rows = xT.rearrange("(p j) t -> p j t", j=PACK)
        raws = [keep.tile([P, 2, chunk[2]], F32, name=f"raw{i}") for i, chunk in enumerate(CHUNKS)]

        def load_x(i):
            u, c0, cols, unused = CHUNKS[i]
            nc.sync.dma_start(raws[i][:], x_rows[:, 2 * u : 2 * u + 2, c0 : c0 + cols])

        def load_scales(q):
            nc.sync.dma_start(w_scales[32 * q : 32 * q + 4, :].bitcast(I32), w1_scales[0, 4 * q : 4 * q + 4, :].bitcast(I32))

        nc.gpsimd.memset(w_scales[:].bitcast(I32), 0)
        nc.sync.dma_start(mem_sb[0][:], mem[0:P, :])
        nc.sync.dma_start(slot_sb[:], slot)
        for a, weight in enumerate((new, old)):
            nc.sync.dma_start(weight_rows[64 * a : 64 * (a + 1), :], weight.rearrange("r (u c) -> (r u) c", c=P)[0:64, :])
        nc.sync.dma_start(offs_sb[:], offs)
        load_x(0)
        load_scales(0)
        load_x(1)
        load_x(2)
        for q in range(1, 4):
            load_scales(q)
        for i in range(3, len(CHUNKS)):
            load_x(i)
        nc.sync.dma_start(w_words[:].bitcast(I32), w1_words[0].bitcast(I32))
        nc.sync.dma_start(mem_sb[1][:], mem[P : 2 * P, :])

        ident = keep.tile([P, P], F32, name="ident")
        make_identity(nc, ident[:])

        weight_cols = keep.tile([P, 2, S // P], F32, name="weight_cols")
        turned_weights = bank(0)
        nc.tensor.transpose(turned_weights[:, 0, :], weight_rows[:], ident[:])
        nc.vector.tensor_copy(weight_cols[:], turned_weights[:, 0, :].rearrange("p (a c) -> p a c", a=2)[:, :, 0 : S // P])

        kept = [[keep.tile([P, 4, P], F32, name=f"kept{b}{h}") for h in range(S // BANK)] for b in range(blocks)]

        def gather_mem(b, h):
            looked = keep.tile([P, BANK], F32, name=f"looked{b}{h}")
            nc.vector.tensor_copy(looked[:], mem_sb[b][:].indirect(slot_sb[:, h * BANK // 16 : (h + 1) * BANK // 16]))
            return looked

        def weigh_mem(b, h, looked, turned):
            for t in range(4):
                nc.tensor.transpose(turned[:, t, :], looked[:, P * t : P * (t + 1)], ident[:])
            old_cols = weight_cols[:, 1, 4 * h : 4 * h + 4]
            if b == 0:
                nc.vector.tensor_tensor(kept[b][h][:], turned[:], old_cols.unsqueeze(2).to_broadcast([P, 4, P]), MULT)
            else:
                for t in range(4):
                    nc.scalar.activation(kept[b][h][:, t, :], turned[:, t, :], COPY, scale=old_cols[:, t : t + 1])

        pairs = [keep.tile([P, T, 2], BF16, name=f"pairs{u}") for u in range(2)]
        picked = [keep.tile([P, 2 * n], U32, name=f"picked{s}", align_bytes=64) for s, (j0, n) in enumerate(SLICES)]

        def round_chunk(i):
            u, c0, cols, s_cols = CHUNKS[i]
            src = raws[i][:].rearrange("p e c -> p c e")
            if s_cols > 0:
                nc.scalar.copy(pairs[u][:, c0 : c0 + s_cols, :], src[:, 0:s_cols, :])
            if s_cols < cols:
                nc.vector.tensor_copy(pairs[u][:, c0 + s_cols : c0 + cols, :], src[:, s_cols:cols, :])

        def gather_pairs(u, s):
            j0, n = SLICES[s]
            window = pairs[u][:].rearrange("p t e -> p (t e)").bitcast(U32)
            nc.vector.tensor_copy(picked[s][:, u * n : (u + 1) * n], window.indirect(offs_sb[:, j0 // 16 : (j0 + n) // 16]))

        first = [gather_mem(0, h) for h in range(2)]
        for h in range(2):
            weigh_mem(0, h, first[h], bank(1 + h))
        round_chunk(0)
        round_chunk(1)
        round_chunk(2)
        for s in range(len(SLICES)):
            gather_pairs(0, s)

        for i in range(3, len(CHUNKS)):
            round_chunk(i)

        def quantize(s, woven):
            j0, n = SLICES[s]
            nc.scalar.copy(woven.rearrange("p (c u) -> p c u", u=2), picked[s][:].rearrange("p (u c) -> p c u", u=2))
            pw = keep.tile([P, n], U32, name=f"pw{s}", align_bytes=64)
            ps = keep.tile([P, n], U8, name=f"ps{s}", align_bytes=64)
            nc.vector.quantize_mx(out=pw[:].bitcast(FP8X4), scales=ps[:], in_=woven.bitcast(BF16))
            return pw, ps

        scaled = [keep.tile([P, N], F32, name=f"scaled{t}") for t in range(S // P)]

        def project(t0, pw, ps, first_col, target):
            acc = target[:].rearrange("p (e b) m -> p e (b m)", e=2)
            for e in range(2):
                cols = slice(first_col + P * e, first_col + P * (e + 1))
                nc.tensor.matmul_mx(
                    out=acc[:, e, :],
                    lhsT=pw[:, cols].bitcast(FP8X4),
                    lhsT_scale=ps[:, cols],
                    rhs=w_words[:].bitcast(FP4X4),
                    rhs_scale=w_scales[:],
                    start=True,
                    stop=True,
                )
            for e in range(2):
                nc.scalar.activation(scaled[t0 + e][:], acc[:, e, :], COPY, scale=weight_cols[:, 0, t0 + e : t0 + e + 1])

        def combine(b, t0, tiles, total):
            old_terms = [kept[b][(t0 + i) // 4][:, (t0 + i) % 4, :] for i in range(tiles)]
            new_terms = [scaled[t0 + i][:, P * b : P * (b + 1)] for i in range(tiles)]
            terms = old_terms + new_terms if b == 0 else new_terms + old_terms
            for i, term in enumerate(terms):
                nc.tensor.matmul(total[:, i % tiles, :], term, ident[:], start=(i == 0), stop=(i == len(terms) - 1), is_transpose=True)
            update = keep.tile([P, tiles * P], F32, name=f"update{b}{t0}")
            nc.scalar.copy(update[:], total[:, 0:tiles, :].rearrange("p i j -> p (i j)"))
            return b, t0, tiles, update

        woven = [keep.tile([P, 2 * n], U32, name=f"woven{s}", align_bytes=64) for s, (j0, n) in enumerate(SLICES)]
        for s in range(len(SLICES)):
            gather_pairs(1, s)
        codes_a = quantize(0, woven[0][:])
        codes_b = quantize(1, woven[1][:])
        looked_0 = gather_mem(1, 0)
        looked_1 = gather_mem(1, 1)
        codes_c = quantize(2, woven[2][:])

        updates = []
        project(0, *codes_a, 0, bank(0))
        updates.append(combine(0, 0, 2, bank(1)))
        project(2, *codes_b, 0, bank(2))
        updates.append(combine(0, 2, 2, bank(3)))
        weigh_mem(1, 0, looked_0, bank(1))
        updates.append(combine(1, 0, 4, bank(4)))
        project(4, *codes_c, 0, bank(3))
        project(6, *codes_c, 2 * P, bank(0))
        updates.append(combine(0, 4, 4, bank(5)))
        weigh_mem(1, 1, looked_1, bank(4))
        updates.append(combine(1, 4, 4, bank(6)))

        for b, t0, tiles, update in updates:
            lst = slot_sb[:, t0 * P // 16 : (t0 + tiles) * P // 16]
            nc.vector.tensor_copy(mem_sb[b][:].indirect(lst), update[:])
        nc.sync.dma_start(out[0:P, :], mem_sb[0][:])
        nc.sync.dma_start(out[P : 2 * P, 0 : U // 2], mem_sb[1][:, 0 : U // 2])
        nc.scalar.dma_start(out[P : 2 * P, U // 2 : U], mem_sb[1][:, U // 2 : U])
